import numpy as np
import ml_dtypes


def mxq(x, axis, fmt="e4m3"):
    dtype, down = {"e4m3": (ml_dtypes.float8_e4m3fn, 7), "e5m2": (ml_dtypes.float8_e5m2, 14)}[fmt]
    v = np.moveaxis(np.asarray(x, np.float32).astype(ml_dtypes.bfloat16).astype(np.float64), axis, -1)
    blocks = v.reshape(v.shape[:-1] + (-1, 32))
    amax = np.abs(blocks).max(-1, keepdims=True)
    byte = np.maximum(np.where(amax > 0, np.frexp(amax)[1] - 1 + 127, 0) - down, 1)
    scale = np.exp2(byte - 127.0)
    codes = (blocks / scale).astype(np.float32).astype(dtype).astype(np.float64)
    return np.moveaxis((codes * scale).reshape(v.shape), -1, axis)


WIDE = False


def mx_kscale(k):
    if not WIDE:
        return np.ones(k)
    levels = np.array([10, -10, 5, -5, 0])
    if k % 512:
        return np.exp2(np.random.permutation(np.resize(levels, k // 32))).repeat(32)
    a = np.empty((k // 512, 16))
    for p in range(k // 512):
        a[p, :8] = np.random.permutation(np.resize(levels, 8))
        for g in range(8):
            far = levels[np.abs(levels - a[p, g]) >= 10]
            a[p, g + 8] = far[np.random.randint(len(far))]
    return np.exp2(a.ravel()).repeat(32)


def f64(x):
    return np.asarray(x).astype(np.float64)


def striped(idx):
    return np.tile(idx.reshape(-1, 16).T, (8, 1)).astype(np.uint16)


def unstriped(offs):
    return offs[:16].T.reshape(-1).astype(np.int64)


def striped8(idx):
    return np.concatenate([x.reshape(-1, 16).T for x in idx]).astype(np.uint16)


def runs(offs, k):
    lists = np.stack([offs[16 * r : 16 * r + 16].T.reshape(-1) for r in range(8)]).astype(np.int64)
    return lists[np.arange(k) % 512 // 64]


def pack_weight(w):
    k, n = w.shape
    w = f64(np.asarray(w, np.float32).astype(ml_dtypes.bfloat16)).reshape(k // 32, 32, n)
    amax = np.abs(w).max(1)
    byte = np.clip(np.where(amax > 0, np.frexp(amax)[1] - 1 + 127 - 7, 1), 1, 254)
    scaled = (w * np.exp2(127.0 - byte)[:, None, :]).reshape(k, n).astype(np.float32)
    words = np.ascontiguousarray(scaled.reshape(k // 512, 128, 4, n).transpose(0, 1, 3, 2)).astype(ml_dtypes.float8_e4m3fn).view(np.uint8)
    return words, np.ascontiguousarray(byte.astype(np.uint8).reshape(k // 512, 16, n))


def unpack_weight(words, scales):
    g, p, n, _ = words.shape
    vals = np.ascontiguousarray(words).view(ml_dtypes.float8_e4m3fn).astype(np.float64) * np.repeat(np.exp2(scales.astype(np.float64) - 127.0), 8, axis=1)[..., None]
    return vals.transpose(0, 1, 3, 2).reshape(g * 512, n)


E2M1 = np.array([0.0, 0.5, 1.0, 1.5, 2.0, 3.0, 4.0, 6.0, -0.0, -0.5, -1.0, -1.5, -2.0, -3.0, -4.0, -6.0])


def pack_fp4(w):
    k, n = w.shape
    w = f64(np.asarray(w, np.float32).astype(ml_dtypes.bfloat16)).reshape(k // 32, 32, n)
    amax = np.abs(w).max(1)
    mant, ex = np.frexp(amax / 6.0)
    byte = np.clip(np.where(amax > 0, np.where(mant > 0.5, ex, ex - 1) + 127, 1), 1, 254)
    scaled = (w * np.exp2(127.0 - byte)[:, None, :]).reshape(k, n).astype(np.float32)
    c = np.ascontiguousarray(scaled.reshape(k // 512, 128, 4, n).transpose(0, 1, 3, 2)).astype(ml_dtypes.float4_e2m1fn).view(np.uint8) & 0xF
    words = (c[..., 0::2] | (c[..., 1::2] << 4)).reshape(k // 512, 128, 2 * n)
    return np.ascontiguousarray(words), np.ascontiguousarray(byte.astype(np.uint8).reshape(k // 512, 16, n))


def unpack_fp4(words, scales):
    g, _, n = scales.shape
    words = np.ascontiguousarray(words).reshape(g, 128, n, 2)
    nib = np.empty((g, 128, n, 4), np.uint8)
    nib[..., 0::2] = words & 0xF
    nib[..., 1::2] = words >> 4
    vals = E2M1[nib] * np.repeat(np.exp2(scales.astype(np.float64) - 127.0), 8, axis=1)[..., None]
    return vals.transpose(0, 1, 3, 2).reshape(g * 512, n)


def planes(y):
    n, m = y.shape
    v = y.astype(np.float32).astype(ml_dtypes.bfloat16).astype(np.float64).reshape(n // 32, 32, m)
    top = np.abs(v).max(1)
    byte = np.clip(np.where(top > 0, np.frexp(top)[1] - 1 + 127 - 7, 1), 1, 254)
    codes = (v * np.exp2(127.0 - byte)[:, None, :]).reshape(n, m).astype(np.float32).astype(ml_dtypes.float8_e4m3fn).view(np.uint8)
    words = codes.reshape(n // 512, 128, 4, m).transpose(0, 1, 3, 2)
    return np.ascontiguousarray(words), np.ascontiguousarray(byte.astype(np.uint8).reshape(n // 512, 16, m))


K, T, S, N, H, J = 512, 2048, 512, 512, 512, 512


def setup_inputs():
    n = np.random.standard_normal
    s = mx_kscale(K)[:, None]
    u = mx_kscale(H)
    packed_xT = pack_weight(n((K, T)) * s)
    packed_w1 = pack_fp4(n((K, H)) / np.sqrt(K) / s)
    packed_w2 = pack_fp4(n((K, H)) / np.sqrt(K) / s)
    packed_w3 = pack_fp4(n((H, H)) / np.sqrt(H) / u[:, None])
    packed_w4 = pack_fp4(n((H, N)) / np.sqrt(H) / u[:, None])
    return {
        "x_words": packed_xT[0],
        "x_scales": packed_xT[1],
        "w1_words": packed_w1[0],
        "w1_scales": packed_w1[1],
        "w2_words": packed_w2[0],
        "w2_scales": packed_w2[1],
        "tab": n((H, J)).astype(np.float32),
        "gn": (np.random.uniform(0.5, 1.5, (H, 1)) * u[:, None]).astype(np.float32),
        "w3_words": packed_w3[0],
        "w3_scales": packed_w3[1],
        "res": (1.5 * n((N, S))).astype(np.float32),
        "w4_words": packed_w4[0],
        "w4_scales": packed_w4[1],
        "offs": striped(np.random.permutation(T)[:S]),
        "two": striped(np.random.permutation(T)[:S]),
        "n1": striped8(np.random.randint(0, J, (8, S))),
        "n2": striped8(np.random.randint(0, J, (8, S))),
        "n3": striped8(np.stack([np.random.permutation(S) for _ in range(8)])),
        "n4": striped8(np.stack([np.random.permutation(S) for _ in range(8)])),
        "n5": striped8(np.stack([np.random.permutation(S) for _ in range(8)])),
        "n6": striped8(np.stack([np.random.permutation(S) for _ in range(8)])),
        "n7": striped8(np.stack([np.random.permutation(S) for _ in range(8)])),
    }


def reference(x_words, x_scales, w1_words, w1_scales, w2_words, w2_scales, tab, gn, w3_words, w3_scales, res, w4_words, w4_scales, offs, two, n1, n2, n3, n4, n5, n6, n7):
    xq = unpack_weight(x_words, x_scales)[:, unstriped(offs)]
    y = unpack_fp4(w1_words, w1_scales).T @ xq
    z = f64(gn) * ((y[np.arange(H)[:, None], runs(n3, H)]) * (f64(tab)[np.arange(H)[:, None], runs(n1, H)]) + f64(tab)[np.arange(H)[:, None], runs(n2, H)])
    h = unpack_fp4(w3_words, w3_scales).T @ mxq(z, 0, "e4m3")
    x_two = unpack_weight(x_words, x_scales)[:, unstriped(two)]
    d = unpack_fp4(w2_words, w2_scales).T @ x_two
    z2 = f64(gn) * (np.maximum(h[np.arange(H)[:, None], runs(n4, H)] + d[np.arange(H)[:, None], runs(n6, H)], h[np.arange(H)[:, None], runs(n5, H)] + d[np.arange(H)[:, None], runs(n7, H)]))
    out_0 = f64(res) + (unpack_fp4(w4_words, w4_scales).T @ mxq(z2, 0, "e4m3"))
    return (out_0,) + planes(out_0)

@@ -1,0 +1,248 @@
+from contextlib import ExitStack
+
+import concourse.mybir as mybir
+from concourse.masks import make_identity
+
+F32 = mybir.dt.float32
+BF16 = mybir.dt.bfloat16
+I32 = mybir.dt.int32
+U32 = mybir.dt.uint32
+U16 = mybir.dt.uint16
+U8 = mybir.dt.uint8
+FP8X4 = mybir.dt.float8_e4m3fn_x4
+FP4X4 = mybir.dt.float4_e2m1fn_x4
+ALU = mybir.AluOpType
+ACT = mybir.ActivationFunctionType
+
+P = 128
+PACK = 4
+S = 512
+TOKENS = 2048
+CHUNKS = S // P
+WIDE = 2 * S
+FLOPS = 4 * 2 * S * S * S
+LAST_PIECES = ((0, 256), (256, 384), (384, 512))
+
+
+def tile_picked_midpathbkinda_none_po_kernel(
+    tc, x_words, x_scales, w1_words, w1_scales, w2_words, w2_scales, tab, gn, w3_words, w3_scales, res,
+    w4_words, w4_scales, offs, two, n1, n2, n3, n4, n5, n6, n7, out_0, out_1, out_2
+):
+    nc = tc.nc
+    with ExitStack() as ctx:
+        keep = ctx.enter_context(tc.tile_pool(name="keep", bufs=1))
+        psum = ctx.enter_context(tc.psum_pool(name="psum", bufs=4))
+
+        def load_list(name, src):
+            tile = keep.tile([P, S // 16], U16, name=name)
+            nc.sync.dma_start(tile[:], src)
+            return tile
+
+        def scale_tile(name, width):
+            tile = keep.tile([P, width], U8, name=name, align_bytes=64)
+            return tile
+
+        def load_scales(queue, tile, src):
+            for q in range(4):
+                queue.dma_start(tile[32 * q : 32 * q + 4, :].bitcast(I32), src[0, 4 * q : 4 * q + 4, :].bitcast(I32))
+
+        def load_weight(name, words):
+            tile = keep.tile([P, 2 * S], U8, name=name, align_bytes=64)
+            nc.sync.dma_start(tile[:].bitcast(I32), words[0].bitcast(I32))
+            return tile
+
+        tab_rows = tab.rearrange("(p t) j -> p t j", t=PACK)
+
+        def load_tab(t):
+            tile = keep.tile([P, WIDE], F32, name="tab%d" % t)
+            nc.sync.dma_start(tile[:, 0:S], tab_rows[:, t, :])
+            return tile
+
+        xs = scale_tile("xs", TOKENS)
+        w1s = scale_tile("w1s", S)
+        w2s = scale_tile("w2s", S)
+        w3s = scale_tile("w3s", S)
+        w4s = scale_tile("w4s", S)
+
+        ident = keep.tile([P, P], F32, name="ident")
+        make_identity(nc, ident[:])
+
+        l1 = load_list("l1", n1)
+        tabs = [load_tab(0)]
+        l_offs = load_list("l_offs", offs)
+        xw = keep.tile([P, TOKENS], U32, name="xw")
+        nc.sync.dma_start(xw[:].bitcast(I32), x_words[0].rearrange("p n r -> p (n r)").bitcast(I32))
+        for q in range(4):
+            rows = x_scales[0, 4 * q : 4 * q + 4, :].bitcast(I32).rearrange("(o r) c -> o r c", o=1)
+            nc.sync.dma_start(xs[32 * q : 32 * q + 32, :].bitcast(I32), rows.to_broadcast([8, 4, TOKENS // 4]))
+        w1 = load_weight("w1", w1_words)
+        load_scales(nc.sync, w1s, w1_scales)
+        tabs.append(load_tab(1))
+        tabs.append(load_tab(2))
+        tabs.append(load_tab(3))
+        l_two = load_list("l_two", two)
+        gain = keep.tile([P, PACK], F32, name="gain")
+        nc.sync.dma_start(gain[:], gn.rearrange("(p t) o -> p (t o)", t=PACK))
+        l3 = load_list("l3", n3)
+        w2 = load_weight("w2", w2_words)
+        load_scales(nc.sync, w2s, w2_scales)
+        l2 = load_list("l2", n2)
+        res_sb = keep.tile([P, PACK, S], F32, name="res_sb")
+        nc.sync.dma_start(res_sb[:], res.rearrange("(p t) j -> p t j", t=PACK))
+        l6 = load_list("l6", n6)
+        l7 = load_list("l7", n7)
+        w3 = load_weight("w3", w3_words)
+        load_scales(nc.sync, w3s, w3_scales)
+        l4 = load_list("l4", n4)
+        l5 = load_list("l5", n5)
+        w4 = load_weight("w4", w4_words)
+        load_scales(nc.sync, w4s, w4_scales)
+
+        def pick_tokens(name, lst):
+            words = keep.tile([P, S], U32, name=name + "_w", align_bytes=64)
+            nc.vector.tensor_copy(words[:], xw[:].indirect(lst[:]))
+            scales = keep.tile([P, S], U8, name=name + "_s", align_bytes=64)
+            nc.vector.tensor_copy(scales[:], xs[:].indirect(lst[:]))
+            return words, scales
+
+        def product_chunk(name, c, codes, scales, w, ws):
+            cols = slice(c * P, (c + 1) * P)
+            bank = psum.tile([P, S], F32, name="bank", tag="product")
+            nc.tensor.matmul_mx(
+                out=bank[:], lhsT=codes[:, cols].bitcast(FP8X4), lhsT_scale=scales[:, cols],
+                rhs=w[:].bitcast(FP4X4), rhs_scale=ws[:], start=True, stop=True,
+            )
+            dealt = keep.tile([P, PACK, P], F32, name="%s_dealt%d" % (name, c))
+            nc.scalar.copy(dealt[:], bank[:].rearrange("j (p t) -> j t p", t=PACK))
+            return dealt
+
+        def turn_back(name, dealt, width, factor):
+            windows = []
+            for t in range(PACK):
+                bank = psum.tile([P, S], F32, name="turned", tag="turned")
+                for c in range(CHUNKS):
+                    nc.tensor.transpose(bank[:, c * P : (c + 1) * P], dealt[c][:, t, :], ident[:])
+                window = keep.tile([P, width], F32, name="%s%d" % (name, t))
+                nc.scalar.activation(window[:, 0:S], bank[:], ACT.Copy, scale=factor[:, t : t + 1])
+                windows.append(window)
+            return windows
+
+        def row_tile(tag):
+            return keep.tile([P, S], F32, name=tag, tag=tag)
+
+        kind1 = [row_tile("kind1_%d" % t) for t in range(PACK)]
+        for t in range(1):
+            nc.vector.tensor_copy(kind1[t][:], tabs[t][:].indirect(l1[:]))
+        xq_w, xq_s = pick_tokens("xq", l_offs)
+        for t in range(1, PACK):
+            nc.vector.tensor_copy(kind1[t][:], tabs[t][:].indirect(l1[:]))
+        x2_w, x2_s = pick_tokens("x2", l_two)
+
+        size = keep.tile([P, PACK], F32, name="size")
+        nc.scalar.activation(size[:], gain[:], ACT.Abs)
+        sign = keep.tile([P, P, PACK], BF16, name="sign")
+        nc.scalar.activation(sign[:], gain[:].rearrange("p (o t) -> p o t", o=1).to_broadcast([P, P, PACK]), ACT.Sign)
+        y = turn_back("y", [product_chunk("y", c, xq_w, xq_s, w1, w1s) for c in range(CHUNKS)], WIDE, gain)
+        tabg = []
+        for t in range(PACK):
+            tile = keep.tile([P, S], F32, name="tabg%d" % t)
+            nc.scalar.activation(tile[:], tabs[t][:, 0:S], ACT.Copy, scale=gain[:, t : t + 1])
+            tabg.append(tile)
+
+        d = turn_back("d", [product_chunk("d", c, x2_w, x2_s, w2, w2s) for c in range(CHUNKS)], WIDE, size)
+
+        res_turned = []
+        for c in range(CHUNKS):
+            bank = psum.tile([P, S], F32, name="bank", tag="product")
+            for t in range(PACK):
+                nc.tensor.transpose(bank[:, t * P : (t + 1) * P], res_sb[:, t, c * P : (c + 1) * P], ident[:])
+            tile = keep.tile([P, PACK, P], F32, name="res_turned%d" % c)
+            nc.scalar.copy(tile[:].rearrange("j t p -> j (t p)"), bank[:])
+            res_turned.append(tile)
+
+        prod = [row_tile("prod_%d" % t) for t in range(PACK)]
+        for t in range(PACK):
+            nc.vector.tensor_tensor(prod[t][:], y[t][:].indirect(l3[:]), kind1[t][:], ALU.mult)
+
+        z_codes = keep.tile([P, S], U32, name="z_codes", align_bytes=64)
+        z_scales = keep.tile([P, S], U8, name="z_scales", align_bytes=64)
+        half = S // 2
+        z_bf = []
+        for a in range(2):
+            cols = slice(a * half, (a + 1) * half)
+            z_half = keep.tile([P, PACK, half], F32, name="z_half", tag="z_half%d" % a)
+            for t in range(PACK):
+                nc.vector.tensor_tensor(
+                    z_half[:, t, :], tabg[t][:].indirect(l2[:, a * half // 16 : (a + 1) * half // 16]), prod[t][:, cols], ALU.add
+                )
+            woven = keep.tile([P, half, PACK], BF16, name="z_bf%d" % a, align_bytes=64)
+            nc.scalar.copy(
+                woven[:].rearrange("p (c i) t -> p c t i", i=2), z_half[:].rearrange("p t (c i) -> p c t i", i=2)
+            )
+            z_bf.append(woven)
+        h_dealt = []
+        for a in range(2):
+            cols = slice(a * half, (a + 1) * half)
+            nc.vector.quantize_mx(
+                out=z_codes[:, cols].bitcast(FP8X4), scales=z_scales[:, cols], in_=z_bf[a][:].rearrange("p j t -> p (j t)")
+            )
+            for c in range(2 * a, 2 * a + 2):
+                h_dealt.append(product_chunk("h", c, z_codes, z_scales, w3, w3s))
+
+        d6 = [row_tile("prod_%d" % t) for t in range(PACK)]
+        for t in range(PACK):
+            nc.vector.tensor_copy(d6[t][:], d[t][:].indirect(l6[:]))
+        d7_pairs = [keep.tile([P, 2, S], F32, name="d7", tag="z_half%d" % a) for a in range(2)]
+        d7 = [d7_pairs[t // 2][:, t % 2, :] for t in range(PACK)]
+        for t in range(PACK):
+            nc.vector.tensor_copy(d7[t], d[t][:].indirect(l7[:]))
+
+        h = turn_back("h", h_dealt, S, size)
+
+        z2_codes = keep.tile([P, S], U32, name="z2_codes", align_bytes=64)
+        z2_scales = keep.tile([P, S], U8, name="z2_scales", align_bytes=64)
+        o_codes = keep.tile([P, S], U32, name="o_codes", align_bytes=64)
+        o_scales = keep.tile([P, S], U8, name="o_scales", align_bytes=64)
+        out_rows = out_0.rearrange("(p t) j -> p t j", t=PACK)
+        out_words = out_1[0].rearrange("p n r -> p (n r)").bitcast(I32)
+
+        for lo, hi in LAST_PIECES:
+            n = hi - lo
+            u = keep.tile([P, PACK, n], F32, name="u%d" % lo)
+            v = keep.tile([P, PACK, n], F32, name="v%d" % lo)
+            for t in range(PACK):
+                nc.vector.tensor_tensor(u[:, t, :], h[t][:].indirect(l4[:, lo // 16 : hi // 16]), d6[t][:, lo:hi], ALU.add)
+                nc.vector.tensor_tensor(v[:, t, :], h[t][:].indirect(l5[:, lo // 16 : hi // 16]), d7[t][:, lo:hi], ALU.add)
+            for c in range(lo // P, hi // P):
+                cols = slice(c * P, (c + 1) * P)
+                part = slice(c * P - lo, (c + 1) * P - lo)
+                larger = keep.tile([P, P, PACK], BF16, name="larger%d" % c)
+                nc.vector.tensor_tensor(
+                    larger[:].rearrange("p (c i) t -> p c t i", i=2),
+                    u[:, :, part].rearrange("p t (c i) -> p c t i", i=2),
+                    v[:, :, part].rearrange("p t (c i) -> p c t i", i=2),
+                    ALU.max,
+                )
+                z2_bf = keep.tile([P, P, PACK], BF16, name="z2_bf%d" % c, align_bytes=64)
+                nc.vector.tensor_tensor(z2_bf[:], larger[:], sign[:], ALU.mult)
+                nc.vector.quantize_mx(
+                    out=z2_codes[:, cols].bitcast(FP8X4), scales=z2_scales[:, cols], in_=z2_bf[:].rearrange("p j t -> p (j t)")
+                )
+                total = psum.tile([P, PACK, P], F32, name="total", tag="turned")
+                for t in range(PACK):
+                    nc.tensor.matmul(total[:, t, :], res_turned[c][:, t, :], ident[:], start=(t == 0), stop=False, is_transpose=True)
+                dealt = product_chunk("o", c, z2_codes, z2_scales, w4, w4s)
+                for t in range(PACK):
+                    nc.tensor.matmul(total[:, t, :], dealt[:, t, :], ident[:], start=False, stop=(t == PACK - 1), is_transpose=True)
+                o_bf = keep.tile([P, P, PACK], BF16, name="o_bf%d" % c, align_bytes=64)
+                nc.scalar.copy(o_bf[:], total[:].rearrange("p t j -> p j t"))
+                o_f32 = keep.tile([P, PACK, P], F32, name="o_f32_%d" % c)
+                nc.scalar.copy(o_f32[:], total[:])
+                nc.sync.dma_start(out_rows[:, :, cols], o_f32[:])
+                nc.vector.quantize_mx(
+                    out=o_codes[:, cols].bitcast(FP8X4), scales=o_scales[:, cols], in_=o_bf[:].rearrange("p j t -> p (j t)")
+                )
+                nc.sync.dma_start(out_words[:, cols], o_codes[:, cols].bitcast(I32))
+        for q in range(4):
+            queue = nc.sync if q % 2 == 0 else nc.scalar
+            queue.dma_start(out_2[0, 4 * q : 4 * q + 4, :].bitcast(I32), o_scales[32 * q : 32 * q + 4, :].bitcast(I32))

@@ -21,6 +21,7 @@ TOKENS = 2048
 CHUNKS = S // P
 WIDE = 2 * S
 FLOPS = 4 * 2 * S * S * S
+EARLY = 2
 LAST_PIECES = ((0, 256), (256, 384), (384, 512))
 
 
@@ -31,7 +32,7 @@ def tile_picked_midpathbkinda_none_po_kernel(
     nc = tc.nc
     with ExitStack() as ctx:
         keep = ctx.enter_context(tc.tile_pool(name="keep", bufs=1))
-        psum = ctx.enter_context(tc.psum_pool(name="psum", bufs=4))
+        psum = ctx.enter_context(tc.psum_pool(name="psum", bufs=1))
 
         def load_list(name, src):
             tile = keep.tile([P, S // 16], U16, name=name)
@@ -58,11 +59,14 @@ def tile_picked_midpathbkinda_none_po_kernel(
             nc.sync.dma_start(tile[:, 0:S], tab_rows[:, t, :])
             return tile
 
+        gain = keep.tile([P, PACK], F32, name="gain")
+        nc.gpsimd.dma_start(gain[:], gn.rearrange("(p t) o -> p (t o)", t=PACK))
         xs = scale_tile("xs", TOKENS)
         w1s = scale_tile("w1s", S)
         w2s = scale_tile("w2s", S)
         w3s = scale_tile("w3s", S)
         w4s = scale_tile("w4s", S)
+        nc.gpsimd.memset(w4s[:].bitcast(I32), 0)
 
         ident = keep.tile([P, P], F32, name="ident")
         make_identity(nc, ident[:])
@@ -70,56 +74,54 @@ def tile_picked_midpathbkinda_none_po_kernel(
         l1 = load_list("l1", n1)
         tabs = [load_tab(0)]
         l_offs = load_list("l_offs", offs)
-        xw = keep.tile([P, TOKENS], U32, name="xw")
-        nc.sync.dma_start(xw[:].bitcast(I32), x_words[0].rearrange("p n r -> p (n r)").bitcast(I32))
         for q in range(4):
             rows = x_scales[0, 4 * q : 4 * q + 4, :].bitcast(I32).rearrange("(o r) c -> o r c", o=1)
             nc.sync.dma_start(xs[32 * q : 32 * q + 32, :].bitcast(I32), rows.to_broadcast([8, 4, TOKENS // 4]))
+        xw = keep.tile([P, TOKENS], U32, name="xw")
+        nc.sync.dma_start(xw[:].bitcast(I32), x_words[0].rearrange("p n r -> p (n r)").bitcast(I32))
         w1 = load_weight("w1", w1_words)
         load_scales(nc.sync, w1s, w1_scales)
         tabs.append(load_tab(1))
         tabs.append(load_tab(2))
         tabs.append(load_tab(3))
         l_two = load_list("l_two", two)
-        gain = keep.tile([P, PACK], F32, name="gain")
-        nc.sync.dma_start(gain[:], gn.rearrange("(p t) o -> p (t o)", t=PACK))
         l3 = load_list("l3", n3)
         w2 = load_weight("w2", w2_words)
         load_scales(nc.sync, w2s, w2_scales)
         l2 = load_list("l2", n2)
-        res_sb = keep.tile([P, PACK, S], F32, name="res_sb")
-        nc.sync.dma_start(res_sb[:], res.rearrange("(p t) j -> p t j", t=PACK))
         l6 = load_list("l6", n6)
         l7 = load_list("l7", n7)
         w3 = load_weight("w3", w3_words)
         load_scales(nc.sync, w3s, w3_scales)
+        res_sb = keep.tile([P, PACK, S], F32, name="res_sb")
+        nc.sync.dma_start(res_sb[:], res.rearrange("(p t) j -> p t j", t=PACK))
         l4 = load_list("l4", n4)
         l5 = load_list("l5", n5)
         w4 = load_weight("w4", w4_words)
         load_scales(nc.sync, w4s, w4_scales)
 
         def pick_tokens(name, lst):
-            words = keep.tile([P, S], U32, name=name + "_w", align_bytes=64)
-            nc.vector.tensor_copy(words[:], xw[:].indirect(lst[:]))
             scales = keep.tile([P, S], U8, name=name + "_s", align_bytes=64)
             nc.vector.tensor_copy(scales[:], xs[:].indirect(lst[:]))
+            words = keep.tile([P, S], U32, name=name + "_w", align_bytes=64)
+            nc.vector.tensor_copy(words[:], xw[:].indirect(lst[:]))
             return words, scales
 
-        def product_chunk(name, c, codes, scales, w, ws):
+        def product_chunk(name, c, codes, scales, w, ws, bank_tag, dealt_tag):
             cols = slice(c * P, (c + 1) * P)
-            bank = psum.tile([P, S], F32, name="bank", tag="product")
+            bank = psum.tile([P, S], F32, name="bank", tag=bank_tag)
             nc.tensor.matmul_mx(
                 out=bank[:], lhsT=codes[:, cols].bitcast(FP8X4), lhsT_scale=scales[:, cols],
                 rhs=w[:].bitcast(FP4X4), rhs_scale=ws[:], start=True, stop=True,
             )
-            dealt = keep.tile([P, PACK, P], F32, name="%s_dealt%d" % (name, c))
+            dealt = keep.tile([P, PACK, P], F32, name="%s_dealt%d" % (name, c), tag=dealt_tag, align_bytes=64)
             nc.scalar.copy(dealt[:], bank[:].rearrange("j (p t) -> j t p", t=PACK))
             return dealt
 
         def turn_back(name, dealt, width, factor):
             windows = []
             for t in range(PACK):
-                bank = psum.tile([P, S], F32, name="turned", tag="turned")
+                bank = psum.tile([P, S], F32, name="turned", tag="turned%d" % t)
                 for c in range(CHUNKS):
                     nc.tensor.transpose(bank[:, c * P : (c + 1) * P], dealt[c][:, t, :], ident[:])
                 window = keep.tile([P, width], F32, name="%s%d" % (name, t))
@@ -129,6 +131,11 @@ def tile_picked_midpathbkinda_none_po_kernel(
 
         def row_tile(tag):
             return keep.tile([P, S], F32, name=tag, tag=tag)
+
+        def scaled_tab(t, tag):
+            tile = keep.tile([P, WIDE], F32, name="tabg%d" % t, tag=tag, align_bytes=64)
+            nc.scalar.activation(tile[:, 0:S], tabs[t][:, 0:S], ACT.Copy, scale=gain[:, t : t + 1])
+            return tile
 
         kind1 = [row_tile("kind1_%d" % t) for t in range(PACK)]
         for t in range(1):
@@ -140,25 +147,13 @@ def tile_picked_midpathbkinda_none_po_kernel(
 
         size = keep.tile([P, PACK], F32, name="size")
         nc.scalar.activation(size[:], gain[:], ACT.Abs)
-        sign = keep.tile([P, P, PACK], BF16, name="sign")
-        nc.scalar.activation(sign[:], gain[:].rearrange("p (o t) -> p o t", o=1).to_broadcast([P, P, PACK]), ACT.Sign)
-        y = turn_back("y", [product_chunk("y", c, xq_w, xq_s, w1, w1s) for c in range(CHUNKS)], WIDE, gain)
-        tabg = []
-        for t in range(PACK):
-            tile = keep.tile([P, S], F32, name="tabg%d" % t)
-            nc.scalar.activation(tile[:], tabs[t][:, 0:S], ACT.Copy, scale=gain[:, t : t + 1])
-            tabg.append(tile)
-
-        d = turn_back("d", [product_chunk("d", c, x2_w, x2_s, w2, w2s) for c in range(CHUNKS)], WIDE, size)
-
-        res_turned = []
-        for c in range(CHUNKS):
-            bank = psum.tile([P, S], F32, name="bank", tag="product")
-            for t in range(PACK):
-                nc.tensor.transpose(bank[:, t * P : (t + 1) * P], res_sb[:, t, c * P : (c + 1) * P], ident[:])
-            tile = keep.tile([P, PACK, P], F32, name="res_turned%d" % c)
-            nc.scalar.copy(tile[:].rearrange("j t p -> j (t p)"), bank[:])
-            res_turned.append(tile)
+        sign = keep.tile([P, 2 * P, PACK], BF16, name="sign")
+        nc.scalar.activation(sign[:], gain[:].rearrange("p (o t) -> p o t", o=1).to_broadcast([P, 2 * P, PACK]), ACT.Sign)
+        tabg = [scaled_tab(0, "tabg0"), scaled_tab(1, "tabg1")]
+        y = turn_back("y", [product_chunk("y", c, xq_w, xq_s, w1, w1s, "product%d" % c, "y_dealt%d" % c) for c in range(CHUNKS)], WIDE, gain)
+        tabg.append(scaled_tab(2, "y_dealt3"))
+        d = turn_back("d", [product_chunk("d", c, x2_w, x2_s, w2, w2s, "product%d" % c, "d_dealt%d" % c) for c in range(CHUNKS)], WIDE, size)
+        tabg.append(scaled_tab(3, "d_dealt0"))
 
         prod = [row_tile("prod_%d" % t) for t in range(PACK)]
         for t in range(PACK):
@@ -166,38 +161,41 @@ def tile_picked_midpathbkinda_none_po_kernel(
 
         z_codes = keep.tile([P, S], U32, name="z_codes", align_bytes=64)
         z_scales = keep.tile([P, S], U8, name="z_scales", align_bytes=64)
-        half = S // 2
-        z_bf = []
-        for a in range(2):
-            cols = slice(a * half, (a + 1) * half)
-            z_half = keep.tile([P, PACK, half], F32, name="z_half", tag="z_half%d" % a)
-            for t in range(PACK):
-                nc.vector.tensor_tensor(
-                    z_half[:, t, :], tabg[t][:].indirect(l2[:, a * half // 16 : (a + 1) * half // 16]), prod[t][:, cols], ALU.add
-                )
-            woven = keep.tile([P, half, PACK], BF16, name="z_bf%d" % a, align_bytes=64)
-            nc.scalar.copy(
-                woven[:].rearrange("p (c i) t -> p c t i", i=2), z_half[:].rearrange("p t (c i) -> p c t i", i=2)
-            )
-            z_bf.append(woven)
-        h_dealt = []
-        for a in range(2):
-            cols = slice(a * half, (a + 1) * half)
-            nc.vector.quantize_mx(
-                out=z_codes[:, cols].bitcast(FP8X4), scales=z_scales[:, cols], in_=z_bf[a][:].rearrange("p j t -> p (j t)")
-            )
-            for c in range(2 * a, 2 * a + 2):
-                h_dealt.append(product_chunk("h", c, z_codes, z_scales, w3, w3s))
-
-        d6 = [row_tile("prod_%d" % t) for t in range(PACK)]
+        z = keep.tile([P, PACK, S], F32, name="z", tag="z")
         for t in range(PACK):
-            nc.vector.tensor_copy(d6[t][:], d[t][:].indirect(l6[:]))
-        d7_pairs = [keep.tile([P, 2, S], F32, name="d7", tag="z_half%d" % a) for a in range(2)]
-        d7 = [d7_pairs[t // 2][:, t % 2, :] for t in range(PACK)]
+            nc.vector.tensor_tensor(z[:, t, :], tabg[t][:].indirect(l2[:]), prod[t][:], ALU.add)
+        z_bf = keep.tile([P, S, PACK], BF16, name="z_bf", tag="d_dealt3", align_bytes=64)
+        nc.scalar.copy(z_bf[:].rearrange("p (c i) t -> p c t i", i=2), z[:].rearrange("p t (c i) -> p c t i", i=2))
+        nc.vector.quantize_mx(out=z_codes[:].bitcast(FP8X4), scales=z_scales[:], in_=z_bf[:].rearrange("p j t -> p (j t)"))
+        h_dealt = [product_chunk("h", c, z_codes, z_scales, w3, w3s, "product%d" % c, "h_dealt%d" % c) for c in range(CHUNKS)]
+
+        w4_dealt = keep.tile([P, 3 * S], U8, name="w4_dealt", tag="d_dealt3", align_bytes=64)
+        nc.gpsimd.tensor_copy(
+            w4_dealt[:, 0 : 2 * S].rearrange("k (t p b) -> k t p b", t=PACK, b=2), w4[:].rearrange("k (p t b) -> k t p b", t=PACK, b=2)
+        )
+        nc.gpsimd.tensor_copy(
+            w4_dealt[:, 2 * S : 3 * S].rearrange("k (t p) -> k t p", t=PACK), w4s[:].rearrange("k (p t) -> k t p", t=PACK)
+        )
+
+        early = [row_tile("prod_%d" % t)[:] for t in range(EARLY)]
+        late = keep.tile([P, 2 * PACK - EARLY, S], F32, name="late", tag="z")
+        picked = early + [late[:, k, :] for k in range(2 * PACK - EARLY)]
+        d6, d7 = picked[:PACK], picked[PACK:]
+        for t in range(PACK):
+            nc.vector.tensor_copy(d6[t], d[t][:].indirect(l6[:]))
         for t in range(PACK):
             nc.vector.tensor_copy(d7[t], d[t][:].indirect(l7[:]))
 
         h = turn_back("h", h_dealt, S, size)
+
+        res_turned = []
+        for c in range(CHUNKS - 1):
+            bank = psum.tile([P, S], F32, name="bank", tag="product%d" % c)
+            for t in range(PACK):
+                nc.tensor.transpose(bank[:, t * P : (t + 1) * P], res_sb[:, t, c * P : (c + 1) * P], ident[:])
+            tile = keep.tile([P, PACK, P], F32, name="res_turned%d" % c, tag="h_dealt%d" % c, align_bytes=64)
+            nc.scalar.copy(tile[:].rearrange("j t p -> j (t p)"), bank[:])
+            res_turned.append(tile)
 
         z2_codes = keep.tile([P, S], U32, name="z2_codes", align_bytes=64)
         z2_scales = keep.tile([P, S], U8, name="z2_scales", align_bytes=64)
@@ -208,36 +206,50 @@ def tile_picked_midpathbkinda_none_po_kernel(
 
         for lo, hi in LAST_PIECES:
             n = hi - lo
-            u = keep.tile([P, PACK, n], F32, name="u%d" % lo)
+            u = keep.tile([P, PACK, n], F32, name="u%d" % lo, tag="piece%d" % lo, align_bytes=64)
             v = keep.tile([P, PACK, n], F32, name="v%d" % lo)
             for t in range(PACK):
                 nc.vector.tensor_tensor(u[:, t, :], h[t][:].indirect(l4[:, lo // 16 : hi // 16]), d6[t][:, lo:hi], ALU.add)
                 nc.vector.tensor_tensor(v[:, t, :], h[t][:].indirect(l5[:, lo // 16 : hi // 16]), d7[t][:, lo:hi], ALU.add)
+            larger = keep.tile([P, n, PACK], BF16, name="larger%d" % lo)
+            nc.vector.tensor_tensor(
+                larger[:].rearrange("p (c i) t -> p c t i", i=2),
+                u[:].rearrange("p t (c i) -> p c t i", i=2),
+                v[:].rearrange("p t (c i) -> p c t i", i=2),
+                ALU.max,
+            )
+            z2_bf = keep.tile([P, n, PACK], BF16, name="z2_bf%d" % lo, tag="piece%d" % hi, align_bytes=64)
+            nc.vector.tensor_tensor(z2_bf[:], larger[:], sign[:, 0:n, :], ALU.mult)
+            nc.vector.quantize_mx(
+                out=z2_codes[:, lo:hi].bitcast(FP8X4), scales=z2_scales[:, lo:hi], in_=z2_bf[:].rearrange("p j t -> p (j t)")
+            )
             for c in range(lo // P, hi // P):
                 cols = slice(c * P, (c + 1) * P)
-                part = slice(c * P - lo, (c + 1) * P - lo)
-                larger = keep.tile([P, P, PACK], BF16, name="larger%d" % c)
-                nc.vector.tensor_tensor(
-                    larger[:].rearrange("p (c i) t -> p c t i", i=2),
-                    u[:, :, part].rearrange("p t (c i) -> p c t i", i=2),
-                    v[:, :, part].rearrange("p t (c i) -> p c t i", i=2),
-                    ALU.max,
-                )
-                z2_bf = keep.tile([P, P, PACK], BF16, name="z2_bf%d" % c, align_bytes=64)
-                nc.vector.tensor_tensor(z2_bf[:], larger[:], sign[:], ALU.mult)
-                nc.vector.quantize_mx(
-                    out=z2_codes[:, cols].bitcast(FP8X4), scales=z2_scales[:, cols], in_=z2_bf[:].rearrange("p j t -> p (j t)")
-                )
-                total = psum.tile([P, PACK, P], F32, name="total", tag="turned")
-                for t in range(PACK):
-                    nc.tensor.matmul(total[:, t, :], res_turned[c][:, t, :], ident[:], start=(t == 0), stop=False, is_transpose=True)
-                dealt = product_chunk("o", c, z2_codes, z2_scales, w4, w4s)
-                for t in range(PACK):
-                    nc.tensor.matmul(total[:, t, :], dealt[:, t, :], ident[:], start=False, stop=(t == PACK - 1), is_transpose=True)
+                total = psum.tile([P, PACK, P], F32, name="total", tag="turned%d" % c)
                 o_bf = keep.tile([P, P, PACK], BF16, name="o_bf%d" % c, align_bytes=64)
-                nc.scalar.copy(o_bf[:], total[:].rearrange("p t j -> p j t"))
                 o_f32 = keep.tile([P, PACK, P], F32, name="o_f32_%d" % c)
-                nc.scalar.copy(o_f32[:], total[:])
+                if c < CHUNKS - 1:
+                    for t in range(PACK):
+                        nc.tensor.matmul(total[:, t, :], res_turned[c][:, t, :], ident[:], start=(t == 0), stop=False, is_transpose=True)
+                    dealt = product_chunk("o", c, z2_codes, z2_scales, w4, w4s, "product%d" % c if c < 2 else "turned0", "o_stage%d" % c)
+                    for t in range(PACK):
+                        nc.tensor.matmul(total[:, t, :], dealt[:, t, :], ident[:], start=False, stop=(t == PACK - 1), is_transpose=True)
+                    nc.scalar.copy(o_bf[:], total[:].rearrange("p t j -> p j t"))
+                    nc.scalar.copy(o_f32[:], total[:])
+                else:
+                    for t in range(PACK):
+                        nc.tensor.matmul_mx(
+                            out=total[:, t, :], lhsT=w4_dealt[:, 2 * P * t : 2 * P * (t + 1)].bitcast(FP4X4),
+                            lhsT_scale=w4_dealt[:, 2 * S + P * t : 2 * S + P * (t + 1)],
+                            rhs=z2_codes[:, cols].bitcast(FP8X4), rhs_scale=z2_scales[:, cols], start=True, stop=True,
+                        )
+                    nc.vector.tensor_tensor(
+                        o_bf[:].rearrange("p (c i) t -> p c t i", i=2),
+                        total[:].rearrange("p t (c i) -> p c t i", i=2),
+                        res_sb[:, :, cols].rearrange("p t (c i) -> p c t i", i=2),
+                        ALU.add,
+                    )
+                    nc.vector.tensor_tensor(o_f32[:], total[:], res_sb[:, :, cols], ALU.add)
                 nc.sync.dma_start(out_rows[:, :, cols], o_f32[:])
                 nc.vector.quantize_mx(
                     out=o_codes[:, cols].bitcast(FP8X4), scales=o_scales[:, cols], in_=o_bf[:].rearrange("p j t -> p (j t)")

@@ -21,7 +21,8 @@ TOKENS = 2048
 CHUNKS = S // P
 WIDE = 2 * S
 FLOPS = 4 * 2 * S * S * S
-EARLY = 2
+HALF = S // 2
+EARLY = 1
 LAST_PIECES = ((0, 256), (256, 384), (384, 512))
 
 
@@ -74,6 +75,7 @@ def tile_picked_midpathbkinda_none_po_kernel(
         l1 = load_list("l1", n1)
         tabs = [load_tab(0)]
         l_offs = load_list("l_offs", offs)
+        l_two = load_list("l_two", two)
         for q in range(4):
             rows = x_scales[0, 4 * q : 4 * q + 4, :].bitcast(I32).rearrange("(o r) c -> o r c", o=1)
             nc.sync.dma_start(xs[32 * q : 32 * q + 32, :].bitcast(I32), rows.to_broadcast([8, 4, TOKENS // 4]))
@@ -84,7 +86,6 @@ def tile_picked_midpathbkinda_none_po_kernel(
         tabs.append(load_tab(1))
         tabs.append(load_tab(2))
         tabs.append(load_tab(3))
-        l_two = load_list("l_two", two)
         l3 = load_list("l3", n3)
         w2 = load_weight("w2", w2_words)
         load_scales(nc.sync, w2s, w2_scales)
@@ -100,12 +101,10 @@ def tile_picked_midpathbkinda_none_po_kernel(
         w4 = load_weight("w4", w4_words)
         load_scales(nc.sync, w4s, w4_scales)
 
-        def pick_tokens(name, lst):
-            scales = keep.tile([P, S], U8, name=name + "_s", align_bytes=64)
-            nc.vector.tensor_copy(scales[:], xs[:].indirect(lst[:]))
-            words = keep.tile([P, S], U32, name=name + "_w", align_bytes=64)
-            nc.vector.tensor_copy(words[:], xw[:].indirect(lst[:]))
-            return words, scales
+        def pick(name, dtype, table, lst):
+            tile = keep.tile([P, S], dtype, name=name, align_bytes=64)
+            nc.vector.tensor_copy(tile[:], table[:].indirect(lst[:]))
+            return tile
 
         def product_chunk(name, c, codes, scales, w, ws, bank_tag, dealt_tag):
             cols = slice(c * P, (c + 1) * P)
@@ -140,10 +139,12 @@ def tile_picked_midpathbkinda_none_po_kernel(
         kind1 = [row_tile("kind1_%d" % t) for t in range(PACK)]
         for t in range(1):
             nc.vector.tensor_copy(kind1[t][:], tabs[t][:].indirect(l1[:]))
-        xq_w, xq_s = pick_tokens("xq", l_offs)
+        xq_s = pick("xq_s", U8, xs, l_offs)
+        x2_s = pick("x2_s", U8, xs, l_two)
+        xq_w = pick("xq_w", U32, xw, l_offs)
         for t in range(1, PACK):
             nc.vector.tensor_copy(kind1[t][:], tabs[t][:].indirect(l1[:]))
-        x2_w, x2_s = pick_tokens("x2", l_two)
+        x2_w = pick("x2_w", U32, xw, l_two)
 
         size = keep.tile([P, PACK], F32, name="size")
         nc.scalar.activation(size[:], gain[:], ACT.Abs)
@@ -164,12 +165,14 @@ def tile_picked_midpathbkinda_none_po_kernel(
         z = keep.tile([P, PACK, S], F32, name="z", tag="z")
         for t in range(PACK):
             nc.vector.tensor_tensor(z[:, t, :], tabg[t][:].indirect(l2[:]), prod[t][:], ALU.add)
-        z_bf = keep.tile([P, S, PACK], BF16, name="z_bf", tag="d_dealt3", align_bytes=64)
-        nc.scalar.copy(z_bf[:].rearrange("p (c i) t -> p c t i", i=2), z[:].rearrange("p t (c i) -> p c t i", i=2))
-        nc.vector.quantize_mx(out=z_codes[:].bitcast(FP8X4), scales=z_scales[:], in_=z_bf[:].rearrange("p j t -> p (j t)"))
+        for a in range(2):
+            cols = slice(a * HALF, (a + 1) * HALF)
+            z_bf = keep.tile([P, HALF, PACK], BF16, name="z_bf%d" % a, tag="d_dealt%d" % (3 - a), align_bytes=64)
+            nc.scalar.copy(z_bf[:].rearrange("p (c i) t -> p c t i", i=2), z[:, :, cols].rearrange("p t (c i) -> p c t i", i=2))
+            nc.vector.quantize_mx(out=z_codes[:, cols].bitcast(FP8X4), scales=z_scales[:, cols], in_=z_bf[:].rearrange("p j t -> p (j t)"))
         h_dealt = [product_chunk("h", c, z_codes, z_scales, w3, w3s, "product%d" % c, "h_dealt%d" % c) for c in range(CHUNKS)]
 
-        w4_dealt = keep.tile([P, 3 * S], U8, name="w4_dealt", tag="d_dealt3", align_bytes=64)
+        w4_dealt = keep.tile([P, 3 * S], U8, name="w4_dealt", tag="d_dealt2", align_bytes=64)
         nc.gpsimd.tensor_copy(
             w4_dealt[:, 0 : 2 * S].rearrange("k (t p b) -> k t p b", t=PACK, b=2), w4[:].rearrange("k (p t b) -> k t p b", t=PACK, b=2)
         )
@@ -178,8 +181,9 @@ def tile_picked_midpathbkinda_none_po_kernel(
         )
 
         early = [row_tile("prod_%d" % t)[:] for t in range(EARLY)]
-        late = keep.tile([P, 2 * PACK - EARLY, S], F32, name="late", tag="z")
-        picked = early + [late[:, k, :] for k in range(2 * PACK - EARLY)]
+        between = keep.tile([P, S], F32, name="between", tag="d_dealt3", align_bytes=64)
+        late = keep.tile([P, 2 * PACK - 2, S], F32, name="late", tag="z")
+        picked = early + [between[:]] + [late[:, k, :] for k in range(2 * PACK - 2)]
         d6, d7 = picked[:PACK], picked[PACK:]
         for t in range(PACK):
             nc.vector.tensor_copy(d6[t], d[t][:].indirect(l6[:]))

from contextlib import ExitStack

import concourse.mybir as mybir
from concourse.masks import make_identity

F32 = mybir.dt.float32
BF16 = mybir.dt.bfloat16
I32 = mybir.dt.int32
U32 = mybir.dt.uint32
U16 = mybir.dt.uint16
U8 = mybir.dt.uint8
FP8X4 = mybir.dt.float8_e4m3fn_x4
FP4X4 = mybir.dt.float4_e2m1fn_x4
ALU = mybir.AluOpType
ACT = mybir.ActivationFunctionType

P = 128
PACK = 4
S = 512
TOKENS = 2048
CHUNKS = S // P
WIDE = 2 * S
FLOPS = 4 * 2 * S * S * S
HALF = S // 2
EARLY = 1
LAST_PIECES = ((0, 256), (256, 384), (384, 512))


def tile_picked_midpathbkinda_none_po_kernel(
    tc, x_words, x_scales, w1_words, w1_scales, w2_words, w2_scales, tab, gn, w3_words, w3_scales, res,
    w4_words, w4_scales, offs, two, n1, n2, n3, n4, n5, n6, n7, out_0, out_1, out_2
):
    nc = tc.nc
    with ExitStack() as ctx:
        keep = ctx.enter_context(tc.tile_pool(name="keep", bufs=1))
        psum = ctx.enter_context(tc.psum_pool(name="psum", bufs=1))

        def load_list(name, src):
            tile = keep.tile([P, S // 16], U16, name=name)
            nc.sync.dma_start(tile[:], src)
            return tile

        def scale_tile(name, width):
            tile = keep.tile([P, width], U8, name=name, align_bytes=64)
            return tile

        def load_scales(queue, tile, src):
            for q in range(4):
                queue.dma_start(tile[32 * q : 32 * q + 4, :].bitcast(I32), src[0, 4 * q : 4 * q + 4, :].bitcast(I32))

        def load_weight(name, words):
            tile = keep.tile([P, 2 * S], U8, name=name, align_bytes=64)
            nc.sync.dma_start(tile[:].bitcast(I32), words[0].bitcast(I32))
            return tile

        tab_rows = tab.rearrange("(p t) j -> p t j", t=PACK)

        def load_tab(t):
            tile = keep.tile([P, WIDE], F32, name="tab%d" % t)
            nc.sync.dma_start(tile[:, 0:S], tab_rows[:, t, :])
            return tile

        gain = keep.tile([P, PACK], F32, name="gain")
        nc.gpsimd.dma_start(gain[:], gn.rearrange("(p t) o -> p (t o)", t=PACK))
        xs = scale_tile("xs", TOKENS)
        w1s = scale_tile("w1s", S)
        w2s = scale_tile("w2s", S)
        w3s = scale_tile("w3s", S)
        w4s = scale_tile("w4s", S)
        nc.gpsimd.memset(w4s[:].bitcast(I32), 0)

        ident = keep.tile([P, P], F32, name="ident")
        make_identity(nc, ident[:])

        l1 = load_list("l1", n1)
        tabs = [load_tab(0)]
        l_offs = load_list("l_offs", offs)
        l_two = load_list("l_two", two)
        for q in range(4):
            rows = x_scales[0, 4 * q : 4 * q + 4, :].bitcast(I32).rearrange("(o r) c -> o r c", o=1)
            nc.sync.dma_start(xs[32 * q : 32 * q + 32, :].bitcast(I32), rows.to_broadcast([8, 4, TOKENS // 4]))
        xw = keep.tile([P, TOKENS], U32, name="xw")
        nc.sync.dma_start(xw[:].bitcast(I32), x_words[0].rearrange("p n r -> p (n r)").bitcast(I32))
        w1 = load_weight("w1", w1_words)
        load_scales(nc.sync, w1s, w1_scales)
        tabs.append(load_tab(1))
        tabs.append(load_tab(2))
        tabs.append(load_tab(3))
        l3 = load_list("l3", n3)
        w2 = load_weight("w2", w2_words)
        load_scales(nc.sync, w2s, w2_scales)
        l2 = load_list("l2", n2)
        l6 = load_list("l6", n6)
        l7 = load_list("l7", n7)
        w3 = load_weight("w3", w3_words)
        load_scales(nc.sync, w3s, w3_scales)
        res_sb = keep.tile([P, PACK, S], F32, name="res_sb")
        nc.sync.dma_start(res_sb[:], res.rearrange("(p t) j -> p t j", t=PACK))
        l4 = load_list("l4", n4)
        l5 = load_list("l5", n5)
        w4 = load_weight("w4", w4_words)
        load_scales(nc.sync, w4s, w4_scales)

        def pick(name, dtype, table, lst):
            tile = keep.tile([P, S], dtype, name=name, align_bytes=64)
            nc.vector.tensor_copy(tile[:], table[:].indirect(lst[:]))
            return tile

        def product_chunk(name, c, codes, scales, w, ws, bank_tag, dealt_tag):
            cols = slice(c * P, (c + 1) * P)
            bank = psum.tile([P, S], F32, name="bank", tag=bank_tag)
            nc.tensor.matmul_mx(
                out=bank[:], lhsT=codes[:, cols].bitcast(FP8X4), lhsT_scale=scales[:, cols],
                rhs=w[:].bitcast(FP4X4), rhs_scale=ws[:], start=True, stop=True,
            )
            dealt = keep.tile([P, PACK, P], F32, name="%s_dealt%d" % (name, c), tag=dealt_tag, align_bytes=64)
            nc.scalar.copy(dealt[:], bank[:].rearrange("j (p t) -> j t p", t=PACK))
            return dealt

        def turn_back(name, dealt, width, factor):
            windows = []
            for t in range(PACK):
                bank = psum.tile([P, S], F32, name="turned", tag="turned%d" % t)
                for c in range(CHUNKS):
                    nc.tensor.transpose(bank[:, c * P : (c + 1) * P], dealt[c][:, t, :], ident[:])
                window = keep.tile([P, width], F32, name="%s%d" % (name, t))
                nc.scalar.activation(window[:, 0:S], bank[:], ACT.Copy, scale=factor[:, t : t + 1])
                windows.append(window)
            return windows

        def row_tile(tag):
            return keep.tile([P, S], F32, name=tag, tag=tag)

        def scaled_tab(t, tag):
            tile = keep.tile([P, WIDE], F32, name="tabg%d" % t, tag=tag, align_bytes=64)
            nc.scalar.activation(tile[:, 0:S], tabs[t][:, 0:S], ACT.Copy, scale=gain[:, t : t + 1])
            return tile

        kind1 = [row_tile("kind1_%d" % t) for t in range(PACK)]
        for t in range(1):
            nc.vector.tensor_copy(kind1[t][:], tabs[t][:].indirect(l1[:]))
        xq_s = pick("xq_s", U8, xs, l_offs)
        x2_s = pick("x2_s", U8, xs, l_two)
        xq_w = pick("xq_w", U32, xw, l_offs)
        for t in range(1, PACK):
            nc.vector.tensor_copy(kind1[t][:], tabs[t][:].indirect(l1[:]))
        x2_w = pick("x2_w", U32, xw, l_two)

        size = keep.tile([P, PACK], F32, name="size")
        nc.scalar.activation(size[:], gain[:], ACT.Abs)
        sign = keep.tile([P, 2 * P, PACK], BF16, name="sign")
        nc.scalar.activation(sign[:], gain[:].rearrange("p (o t) -> p o t", o=1).to_broadcast([P, 2 * P, PACK]), ACT.Sign)
        tabg = [scaled_tab(0, "tabg0"), scaled_tab(1, "tabg1")]
        y = turn_back("y", [product_chunk("y", c, xq_w, xq_s, w1, w1s, "product%d" % c, "y_dealt%d" % c) for c in range(CHUNKS)], WIDE, gain)
        tabg.append(scaled_tab(2, "y_dealt3"))
        d = turn_back("d", [product_chunk("d", c, x2_w, x2_s, w2, w2s, "product%d" % c, "d_dealt%d" % c) for c in range(CHUNKS)], WIDE, size)
        tabg.append(scaled_tab(3, "d_dealt0"))

        prod = [row_tile("prod_%d" % t) for t in range(PACK)]
        for t in range(PACK):
            nc.vector.tensor_tensor(prod[t][:], y[t][:].indirect(l3[:]), kind1[t][:], ALU.mult)

        z_codes = keep.tile([P, S], U32, name="z_codes", align_bytes=64)
        z_scales = keep.tile([P, S], U8, name="z_scales", align_bytes=64)
        z = keep.tile([P, PACK, S], F32, name="z", tag="z")
        for t in range(PACK):
            nc.vector.tensor_tensor(z[:, t, :], tabg[t][:].indirect(l2[:]), prod[t][:], ALU.add)
        for a in range(2):
            cols = slice(a * HALF, (a + 1) * HALF)
            z_bf = keep.tile([P, HALF, PACK], BF16, name="z_bf%d" % a, tag="d_dealt%d" % (3 - a), align_bytes=64)
            nc.scalar.copy(z_bf[:].rearrange("p (c i) t -> p c t i", i=2), z[:, :, cols].rearrange("p t (c i) -> p c t i", i=2))
            nc.vector.quantize_mx(out=z_codes[:, cols].bitcast(FP8X4), scales=z_scales[:, cols], in_=z_bf[:].rearrange("p j t -> p (j t)"))
        h_dealt = [product_chunk("h", c, z_codes, z_scales, w3, w3s, "product%d" % c, "h_dealt%d" % c) for c in range(CHUNKS)]

        w4_dealt = keep.tile([P, 3 * S], U8, name="w4_dealt", tag="d_dealt2", align_bytes=64)
        nc.gpsimd.tensor_copy(
            w4_dealt[:, 0 : 2 * S].rearrange("k (t p b) -> k t p b", t=PACK, b=2), w4[:].rearrange("k (p t b) -> k t p b", t=PACK, b=2)
        )
        nc.gpsimd.tensor_copy(
            w4_dealt[:, 2 * S : 3 * S].rearrange("k (t p) -> k t p", t=PACK), w4s[:].rearrange("k (p t) -> k t p", t=PACK)
        )

        early = [row_tile("prod_%d" % t)[:] for t in range(EARLY)]
        between = keep.tile([P, S], F32, name="between", tag="d_dealt3", align_bytes=64)
        late = keep.tile([P, 2 * PACK - 2, S], F32, name="late", tag="z")
        picked = early + [between[:]] + [late[:, k, :] for k in range(2 * PACK - 2)]
        d6, d7 = picked[:PACK], picked[PACK:]
        for t in range(PACK):
            nc.vector.tensor_copy(d6[t], d[t][:].indirect(l6[:]))
        for t in range(PACK):
            nc.vector.tensor_copy(d7[t], d[t][:].indirect(l7[:]))

        h = turn_back("h", h_dealt, S, size)

        res_turned = []
        for c in range(CHUNKS - 1):
            bank = psum.tile([P, S], F32, name="bank", tag="product%d" % c)
            for t in range(PACK):
                nc.tensor.transpose(bank[:, t * P : (t + 1) * P], res_sb[:, t, c * P : (c + 1) * P], ident[:])
            tile = keep.tile([P, PACK, P], F32, name="res_turned%d" % c, tag="h_dealt%d" % c, align_bytes=64)
            nc.scalar.copy(tile[:].rearrange("j t p -> j (t p)"), bank[:])
            res_turned.append(tile)

        z2_codes = keep.tile([P, S], U32, name="z2_codes", align_bytes=64)
        z2_scales = keep.tile([P, S], U8, name="z2_scales", align_bytes=64)
        o_codes = keep.tile([P, S], U32, name="o_codes", align_bytes=64)
        o_scales = keep.tile([P, S], U8, name="o_scales", align_bytes=64)
        out_rows = out_0.rearrange("(p t) j -> p t j", t=PACK)
        out_words = out_1[0].rearrange("p n r -> p (n r)").bitcast(I32)

        for lo, hi in LAST_PIECES:
            n = hi - lo
            u = keep.tile([P, PACK, n], F32, name="u%d" % lo, tag="piece%d" % lo, align_bytes=64)
            v = keep.tile([P, PACK, n], F32, name="v%d" % lo)
            for t in range(PACK):
                nc.vector.tensor_tensor(u[:, t, :], h[t][:].indirect(l4[:, lo // 16 : hi // 16]), d6[t][:, lo:hi], ALU.add)
                nc.vector.tensor_tensor(v[:, t, :], h[t][:].indirect(l5[:, lo // 16 : hi // 16]), d7[t][:, lo:hi], ALU.add)
            larger = keep.tile([P, n, PACK], BF16, name="larger%d" % lo)
            nc.vector.tensor_tensor(
                larger[:].rearrange("p (c i) t -> p c t i", i=2),
                u[:].rearrange("p t (c i) -> p c t i", i=2),
                v[:].rearrange("p t (c i) -> p c t i", i=2),
                ALU.max,
            )
            z2_bf = keep.tile([P, n, PACK], BF16, name="z2_bf%d" % lo, tag="piece%d" % hi, align_bytes=64)
            nc.vector.tensor_tensor(z2_bf[:], larger[:], sign[:, 0:n, :], ALU.mult)
            nc.vector.quantize_mx(
                out=z2_codes[:, lo:hi].bitcast(FP8X4), scales=z2_scales[:, lo:hi], in_=z2_bf[:].rearrange("p j t -> p (j t)")
            )
            for c in range(lo // P, hi // P):
                cols = slice(c * P, (c + 1) * P)
                total = psum.tile([P, PACK, P], F32, name="total", tag="turned%d" % c)
                o_bf = keep.tile([P, P, PACK], BF16, name="o_bf%d" % c, align_bytes=64)
                o_f32 = keep.tile([P, PACK, P], F32, name="o_f32_%d" % c)
                if c < CHUNKS - 1:
                    for t in range(PACK):
                        nc.tensor.matmul(total[:, t, :], res_turned[c][:, t, :], ident[:], start=(t == 0), stop=False, is_transpose=True)
                    dealt = product_chunk("o", c, z2_codes, z2_scales, w4, w4s, "product%d" % c if c < 2 else "turned0", "o_stage%d" % c)
                    for t in range(PACK):
                        nc.tensor.matmul(total[:, t, :], dealt[:, t, :], ident[:], start=False, stop=(t == PACK - 1), is_transpose=True)
                    nc.scalar.copy(o_bf[:], total[:].rearrange("p t j -> p j t"))
                    nc.scalar.copy(o_f32[:], total[:])
                else:
                    for t in range(PACK):
                        nc.tensor.matmul_mx(
                            out=total[:, t, :], lhsT=w4_dealt[:, 2 * P * t : 2 * P * (t + 1)].bitcast(FP4X4),
                            lhsT_scale=w4_dealt[:, 2 * S + P * t : 2 * S + P * (t + 1)],
                            rhs=z2_codes[:, cols].bitcast(FP8X4), rhs_scale=z2_scales[:, cols], start=True, stop=True,
                        )
                    nc.vector.tensor_tensor(
                        o_bf[:].rearrange("p (c i) t -> p c t i", i=2),
                        total[:].rearrange("p t (c i) -> p c t i", i=2),
                        res_sb[:, :, cols].rearrange("p t (c i) -> p c t i", i=2),
                        ALU.add,
                    )
                    nc.vector.tensor_tensor(o_f32[:], total[:], res_sb[:, :, cols], ALU.add)
                nc.sync.dma_start(out_rows[:, :, cols], o_f32[:])
                nc.vector.quantize_mx(
                    out=o_codes[:, cols].bitcast(FP8X4), scales=o_scales[:, cols], in_=o_bf[:].rearrange("p j t -> p (j t)")
                )
                nc.sync.dma_start(out_words[:, cols], o_codes[:, cols].bitcast(I32))
        for q in range(4):
            queue = nc.sync if q % 2 == 0 else nc.scalar
            queue.dma_start(out_2[0, 4 * q : 4 * q + 4, :].bitcast(I32), o_scales[32 * q : 32 * q + 4, :].bitcast(I32))
